import numpy as np
import ml_dtypes


def mxq(x, axis, fmt="e4m3"):
    dtype, down = {"e4m3": (ml_dtypes.float8_e4m3fn, 7), "e5m2": (ml_dtypes.float8_e5m2, 14)}[fmt]
    v = np.moveaxis(np.asarray(x, np.float32).astype(ml_dtypes.bfloat16).astype(np.float64), axis, -1)
    blocks = v.reshape(v.shape[:-1] + (-1, 32))
    amax = np.abs(blocks).max(-1, keepdims=True)
    byte = np.maximum(np.where(amax > 0, np.frexp(amax)[1] - 1 + 127, 0) - down, 1)
    scale = np.exp2(byte - 127.0)
    codes = (blocks / scale).astype(np.float32).astype(dtype).astype(np.float64)
    return np.moveaxis((codes * scale).reshape(v.shape), -1, axis)


WIDE = False


def mx_kscale(k):
    if not WIDE:
        return np.ones(k)
    levels = np.array([10, -10, 5, -5, 0])
    if k % 512:
        return np.exp2(np.random.permutation(np.resize(levels, k // 32))).repeat(32)
    a = np.empty((k // 512, 16))
    for p in range(k // 512):
        a[p, :8] = np.random.permutation(np.resize(levels, 8))
        for g in range(8):
            far = levels[np.abs(levels - a[p, g]) >= 10]
            a[p, g + 8] = far[np.random.randint(len(far))]
    return np.exp2(a.ravel()).repeat(32)


def f64(x):
    return np.asarray(x).astype(np.float64)


def striped(idx):
    return np.tile(idx.reshape(-1, 16).T, (8, 1)).astype(np.uint16)


def unstriped(offs):
    return offs[:16].T.reshape(-1).astype(np.int64)


E2M1 = np.array([0.0, 0.5, 1.0, 1.5, 2.0, 3.0, 4.0, 6.0, -0.0, -0.5, -1.0, -1.5, -2.0, -3.0, -4.0, -6.0])


def pack_weight(w, fmt):
    k, n = w.shape
    w = f64(np.asarray(w, np.float32).astype(ml_dtypes.bfloat16)).reshape(k // 32, 32, n)
    amax = np.abs(w).max(1)
    if fmt == "e4m3":
        byte = np.frexp(amax)[1] - 1 + 127 - 7
    else:
        mant, ex = np.frexp(amax / 6.0)
        byte = np.where(mant > 0.5, ex, ex - 1) + 127
    byte = np.clip(np.where(amax > 0, byte, 1), 1, 254)
    scaled = (w * np.exp2(127.0 - byte)[:, None, :]).reshape(k, n).astype(np.float32)
    by_word = np.ascontiguousarray(scaled.reshape(k // 512, 128, 4, n).transpose(0, 1, 3, 2))
    if fmt == "e4m3":
        words = by_word.astype(ml_dtypes.float8_e4m3fn).view(np.uint8)
    else:
        c = by_word.astype(ml_dtypes.float4_e2m1fn).view(np.uint8) & 0xF
        words = (c[..., 0::2] | (c[..., 1::2] << 4)).reshape(k // 512, 128, 2 * n)
    return np.ascontiguousarray(words), np.ascontiguousarray(byte.astype(np.uint8).reshape(k // 512, 16, n))


def unpack_weight(words, scales, fmt):
    g, _, n = scales.shape
    words = np.ascontiguousarray(words).reshape(g, 128, n, -1)
    if fmt == "e4m3":
        vals = words.view(ml_dtypes.float8_e4m3fn).astype(np.float64)
    else:
        nib = np.empty((g, 128, n, 4), np.uint8)
        nib[..., 0::2] = words & 0xF
        nib[..., 1::2] = words >> 4
        vals = E2M1[nib]
    vals = vals * np.repeat(np.exp2(scales.astype(np.float64) - 127.0), 8, axis=1)[..., None]
    return vals.transpose(0, 1, 3, 2).reshape(g * 512, n)


def planes(y):
    n, m = y.shape
    v = y.astype(np.float32).astype(ml_dtypes.bfloat16).astype(np.float64).reshape(n // 32, 32, m)
    top = np.abs(v).max(1)
    byte = np.clip(np.where(top > 0, np.frexp(top)[1] - 1 + 127 - 7, 1), 1, 254)
    codes = (v * np.exp2(127.0 - byte)[:, None, :]).reshape(n, m).astype(np.float32).astype(ml_dtypes.float8_e4m3fn).view(np.uint8)
    words = codes.reshape(n // 512, 128, 4, m).transpose(0, 1, 3, 2)
    return np.ascontiguousarray(words), np.ascontiguousarray(byte.astype(np.uint8).reshape(n // 512, 16, m))


K, T, G, C1, E, C2, H = 512, 1024, 2, 512, 8, 128, 512
N = 512


def by_expert(wq, xq, E, C):
    return np.concatenate([wq[e].T @ xq[:, e * C:(e + 1) * C] for e in range(E)], axis=1)


def setup_inputs():
    n = np.random.standard_normal
    s = mx_kscale(K)
    u = mx_kscale(H)
    slots1 = np.random.permutation(T)
    slots2 = np.concatenate([q * C1 + np.random.permutation(C1) for q in range(G)])
    x = pack_weight(n((K, T)) * s[:, None], "e4m3")
    wg = [pack_weight(m, "e4m3") for m in n((G, K, H)) / np.sqrt(K) / s[None, :, None] * u]
    we = [pack_weight(m, "e4m3") for m in n((E, H, N)) / np.sqrt(H) / u[None, :, None]]
    return {
        "x_words": x[0],
        "x_scales": x[1],
        "wg_words": np.stack([m[0] for m in wg]),
        "wg_scales": np.stack([m[1] for m in wg]),
        "we_words": np.stack([m[0] for m in we]),
        "we_scales": np.stack([m[1] for m in we]),
        "gate": (np.tile(np.random.uniform(0.2, 1.0, T), (128, 1))).astype(np.float32),
        "offs": striped(slots1),
        "offs2": striped(slots2),
        "dst": striped(slots1[slots2]),
    }


def reference(x_words, x_scales, wg_words, wg_scales, we_words, we_scales, gate, offs, offs2, dst):
    wg = np.stack([unpack_weight(wg_words[e], wg_scales[e], "e4m3") for e in range(G)])
    we = np.stack([unpack_weight(we_words[e], we_scales[e], "e4m3") for e in range(E)])
    idx, idx2 = unstriped(offs), unstriped(offs2)
    xq = unpack_weight(x_words, x_scales, "e4m3")[:, idx]
    a = by_expert(wg, xq, G, C1)
    y = by_expert(we, mxq(a[:, idx2], 0, "e4m3"), E, C2)
    out = np.zeros((N, T))
    out[:, unstriped(dst)] = f64(gate[:1]) * y
    out_0 = out
    return (out_0,) + planes(out_0)

@@ -1,0 +1,259 @@
+from contextlib import ExitStack
+
+import concourse.mybir as mybir
+from concourse.masks import make_identity
+
+K, T, G, C1, E, C2, H, N = 512, 1024, 2, 512, 8, 128, 512, 512
+FLOPS = 2 * K * H * T + 2 * H * N * T
+
+F32 = mybir.dt.float32
+BF16 = mybir.dt.bfloat16
+I32 = mybir.dt.int32
+U32 = mybir.dt.uint32
+U16 = mybir.dt.uint16
+U8 = mybir.dt.uint8
+FP8X4 = mybir.dt.float8_e4m3fn_x4
+COPY = mybir.ActivationFunctionType.Copy
+
+P = 128
+PACK = 4
+QUADS = 4
+LANES = 16
+HALF = T // 2
+
+
+def tile_moe_hie_none_kernel(
+    tc, x_words, x_scales, wg_words, wg_scales, we_words, we_scales, gate, offs, offs2, dst, out_0, out_1, out_2
+):
+    nc = tc.nc
+    with ExitStack() as ctx:
+        keep = ctx.enter_context(tc.tile_pool(name="keep", bufs=1))
+        ring = ctx.enter_context(tc.tile_pool(name="ring", bufs=4))
+        psum = ctx.enter_context(tc.psum_pool(name="psum", bufs=1))
+
+        def bank(number, shape, dtype=F32):
+            return psum.tile(shape, dtype, name=f"bank{number}")
+
+        def held(shape, dtype, name):
+            return keep.tile(shape, dtype, name=name, align_bytes=64)
+
+        def entries(lst, first, count):
+            return lst[:, first // LANES : (first + count) // LANES]
+
+        def quad_rows(plane, q):
+            return plane[32 * q : 32 * q + 4].bitcast(I32)
+
+        offs_t = keep.tile([P, T // LANES], U16, name="offs_t")
+        offs2_t = keep.tile([P, T // LANES], U16, name="offs2_t")
+        dst_t = keep.tile([P, T // LANES], U16, name="dst_t")
+
+        xw = held([P, T], I32, "xw")
+        xs = held([P, T], U8, "xs")
+        wgw = [held([P, H], I32, f"wgw{f}") for f in range(G)]
+        wgs = held([P, G, H], U8, "wgs")
+        wes = held([P, E, N], U8, "wes")
+        gate_rows = held([P, P], F32, "gate_rows")
+        a_planes = keep.tile([P, PACK + 1, C1], BF16, name="a_planes", tag="late", align_bytes=64)
+        ident = held([P, P], F32, "ident")
+        ident_bf = held([P, P], BF16, "ident_bf")
+
+        nc.gpsimd.memset(xs[:].bitcast(I32), 0)
+        nc.vector.memset(wgs[:].bitcast(I32), 0)
+        nc.vector.memset(gate_rows[:], 0.0)
+        nc.vector.memset(wes[:].bitcast(I32), 0)
+        nc.vector.memset(a_planes[:, 0, :], 0.0)
+        make_identity(nc, ident[:])
+        nc.scalar.copy(ident_bf[:], ident[:])
+
+        def load_group(f):
+            nc.sync.dma_start(wgw[f][:], wg_words[f][0].rearrange("p i d -> p (i d)").bitcast(I32))
+
+        we_cols = we_words.rearrange("e s p n d -> (s p) e (n d)").bitcast(I32)
+        wew = []
+
+        def load_experts(first, count):
+            part = held([P, count, N], I32, f"wew{first}")
+            nc.sync.dma_start(part[:], we_cols[:, first : first + count, :])
+            wew.extend(part[:, j, :] for j in range(count))
+
+        nc.sync.dma_start(offs_t[:], offs)
+        nc.sync.dma_start(offs2_t[:], offs2)
+        nc.sync.dma_start(dst_t[:], dst)
+        for q in range(QUADS):
+            if q == 2:
+                nc.sync.dma_start(xw[:], x_words[0].rearrange("p t d -> p (t d)").bitcast(I32))
+            nc.sync.dma_start(quad_rows(xs, q), x_scales[0][4 * q : 4 * q + 4].bitcast(I32))
+        load_group(0)
+        wg_rows = wg_scales.rearrange("f s b i -> (s b) f i")
+        for q in range(QUADS):
+            nc.sync.dma_start(quad_rows(wgs, q), wg_rows[4 * q : 4 * q + 4].bitcast(I32))
+        nc.sync.dma_start(gate_rows[0:E, :], gate[0:1, :].rearrange("r (e m) -> (r e) m", e=E))
+        load_group(1)
+        we_rows = we_scales.rearrange("e s b n -> (s b) e n")
+        for q in range(QUADS):
+            nc.sync.dma_start(quad_rows(wes, q), we_rows[4 * q : 4 * q + 4].bitcast(I32))
+        for first, count in ((0, 1), (1, 1), (2, 2), (4, 2), (6, 2)):
+            load_experts(first, count)
+
+        def gather_tokens(first, count):
+            words = held([P, count], U32, f"xgw{first}")
+            scales = held([P, count], U8, f"xgs{first}")
+            nc.vector.tensor_copy(words[:], xw[:].bitcast(U32).indirect(entries(offs_t, first, count)))
+            nc.vector.tensor_copy(scales[:], xs[:].indirect(entries(offs_t, first, count)))
+            return [(words[:, c : c + P], scales[:, c : c + P]) for c in range(0, count, P)]
+
+        def group_layer(block, f, acc):
+            words, scales = block
+            nc.tensor.matmul_mx(
+                out=acc[:],
+                lhsT=words.bitcast(FP8X4),
+                lhsT_scale=scales,
+                rhs=wgw[f][:].bitcast(FP8X4),
+                rhs_scale=wgs[:, f, :],
+                start=True,
+                stop=True,
+            )
+            return acc
+
+        a_pairs = held([P, 2, C1], F32, "a_pairs")
+        blocks0 = gather_tokens(0, 128) + gather_tokens(128, 128) + gather_tokens(256, 256)
+        turned = [bank(4 + u, [P, C1]) for u in range(2)]
+        for b in range(4):
+            acc = group_layer(blocks0[b], 0, bank(b, [P, H]))
+            rows = ring.tile([P, H], BF16, name="rows", align_bytes=64)
+            nc.scalar.copy(
+                rows[:].rearrange("m (u p e) -> m u p e", u=2, e=2),
+                acc[:].rearrange("m (p u e) -> m u p e", u=2, e=2),
+            )
+            pairs = rows[:].bitcast(F32)
+            for u in range(2):
+                nc.tensor.transpose(turned[u][:, b * P : (b + 1) * P], pairs[:, u * P : (u + 1) * P], ident[:])
+
+        blocks1 = gather_tokens(C1, C1)
+        nc.scalar.copy(a_pairs[:, 0, :], turned[0][:])
+        nc.vector.tensor_copy(a_pairs[:, 1, :], turned[1][:])
+
+        gate_ps = bank(6, [P, P])
+        nc.tensor.transpose(gate_ps[:], gate_rows[:], ident[:])
+        gate_cols = held([P, E], F32, "gate_cols")
+        nc.scalar.copy(gate_cols[:], gate_ps[:, 0:E])
+
+
+        def quantise(grouped, count, name):
+            codes = held([P, count], U32, f"codes_{name}")
+            scales = held([P, count], U8, f"scales_{name}")
+            nc.vector.quantize_mx(out=codes[:].bitcast(FP8X4), scales=scales[:], in_=grouped[:])
+            return codes, scales
+
+        def regather_pairs(first, count):
+            grouped = held([P, PACK * count], BF16, f"grouped{first}")
+            as_pairs = grouped[:].bitcast(U32).rearrange("p (m u) -> p m u", u=2)
+            for u in range(2):
+                window = a_pairs[:, u, :].bitcast(U32)
+                nc.vector.tensor_copy(as_pairs[:, :, u], window.indirect(entries(offs2_t, first, count)))
+            return grouped
+
+        def regather_planes(first, count):
+            grouped = held([P, PACK * count], BF16, f"grouped{first}")
+            by_plane = grouped[:].rearrange("p (m t) -> p m t", t=PACK)
+            flat = a_planes[:].rearrange("p s c -> p (s c)")
+            for t in range(PACK):
+                window = flat[:, t * C1 : (t + 2) * C1]
+                nc.scalar.activation(by_plane[:, :, t], window.indirect(entries(offs2_t, first, count)), COPY)
+            return grouped
+
+        def expert_rows(e, quantised, col):
+            codes, scales = quantised
+            acc = bank(e % 2 if e < 4 else e - 4, [P, N])
+            nc.tensor.matmul_mx(
+                out=acc[:],
+                lhsT=codes[:, col : col + P].bitcast(FP8X4),
+                lhsT_scale=scales[:, col : col + P],
+                rhs=wew[e].bitcast(FP8X4),
+                rhs_scale=wes[:, e, :],
+                start=True,
+                stop=True,
+            )
+            gated = ring.tile([P, PACK, P], F32, name="gated")
+            nc.scalar.activation(
+                gated[:], acc[:].rearrange("m (p t) -> m t p", t=PACK), COPY, scale=gate_cols[:, e : e + 1]
+            )
+            return gated
+
+        planes = [keep.tile([P, T], F32, name=f"plane{t}") for t in range(PACK)]
+
+        def expert_by_slots(e, quantised, col):
+            gated = expert_rows(e, quantised, col)
+            turned = bank((2, 3, 7, 6)[e], [P, PACK, P])
+            if e < 3:
+                y = held([P, PACK, P], F32, f"y{e}")
+            else:
+                y = keep.tile([P, PACK, P], F32, name="y3", tag="late", align_bytes=64)
+            for t in range(PACK):
+                nc.tensor.transpose(turned[:, t, :], gated[:, t, :], ident[:])
+            nc.scalar.copy(y[:], turned[:])
+            for t in range(PACK):
+                nc.vector.tensor_copy(planes[t][:].indirect(entries(dst_t, e * C2, C2)), y[:, t, :])
+
+        q0 = quantise(regather_pairs(0, C2), C2, "e0")
+        q1 = quantise(regather_pairs(C2, C2), C2, "e1")
+        q23 = quantise(regather_pairs(2 * C2, 2 * C2), 2 * C2, "e23")
+        expert_by_slots(0, q0, 0)
+        expert_by_slots(1, q1, 0)
+
+        for b in range(4):
+            acc = group_layer(blocks1[b], 1, bank((4, 5, 0, 1)[b], [P, H]))
+            rows = ring.tile([P, H], BF16, name="rows", align_bytes=64)
+            nc.scalar.copy(
+                rows[:].rearrange("m (t p) -> m t p", t=PACK), acc[:].rearrange("m (p t) -> m t p", t=PACK)
+            )
+            turned = bank(6 + b % 2, [P, PACK, P], BF16)
+            for t in range(PACK):
+                nc.tensor.transpose(turned[:, t, :], rows[:, t * P : (t + 1) * P], ident_bf[:])
+            nc.scalar.copy(a_planes[:, 1:, b * P : (b + 1) * P], turned[:])
+
+        q45 = quantise(regather_planes(C1, 2 * C2), 2 * C2, "e45")
+        expert_by_slots(2, q23, 0)
+        q67 = quantise(regather_planes(C1 + 2 * C2, 2 * C2), 2 * C2, "e67")
+        expert_by_slots(3, q23, C2)
+
+        banks = [bank(4 + t, [P, C1]) for t in range(PACK)]
+        for j in range(4):
+            gated = expert_rows(4 + j, (q45, q67)[j // 2], (j % 2) * C2)
+            for t in range(PACK):
+                nc.tensor.transpose(banks[t][:, j * P : (j + 1) * P], gated[:, t, :], ident[:])
+        ys = []
+        for t in range(PACK):
+            y = held([P, C1], F32, f"y1_{t}")
+            nc.scalar.copy(y[:], banks[t][:])
+            ys.append(y)
+
+        rounded = [held([P, HALF, PACK], BF16, f"rounded{h}") for h in range(2)]
+        last_pair = held([P, 2, HALF], BF16, "last_pair")
+        out_rows = out_0.rearrange("(p t) c -> p t c", t=PACK)
+        for t in range(PACK):
+            nc.vector.tensor_copy(planes[t][:].indirect(entries(dst_t, C1, C1)), ys[t][:])
+            nc.sync.dma_start(out_rows[:, t, :], planes[t][:])
+            if t < 2:
+                nc.scalar.copy(rounded[0][:, :, t], planes[t][:, 0:HALF])
+            elif t == 2:
+                nc.scalar.copy(last_pair[:, 0, :], planes[t][:, 0:HALF])
+            else:
+                nc.vector.tensor_copy(last_pair[:, 1, :], planes[t][:, 0:HALF])
+                nc.vector.tensor_copy(rounded[0][:, :, 2:4], last_pair[:].rearrange("p e m -> p m e"))
+            nc.scalar.copy(rounded[1][:, :, t], planes[t][:, HALF:T])
+
+        out_scales = held([P, T], U8, "out_scales")
+        out_words = out_1[0].rearrange("p t d -> p (t d)").bitcast(I32)
+        for h in range(2):
+            cols = slice(h * HALF, (h + 1) * HALF)
+            codes = held([P, HALF], U32, f"out_codes{h}")
+            nc.vector.quantize_mx(
+                out=codes[:].bitcast(FP8X4),
+                scales=out_scales[:, cols],
+                in_=rounded[h][:].rearrange("p m t -> p (m t)"),
+            )
+            nc.sync.dma_start(out_words[:, cols], codes[:].bitcast(I32))
+        for q in range(QUADS):
+            queue = nc.sync if q % 2 else nc.scalar
+            queue.dma_start(out_2[0][4 * q : 4 * q + 4].bitcast(I32), quad_rows(out_scales, q))

@@ -53,17 +53,13 @@ def tile_moe_hie_none_kernel(
         wgs = held([P, G, H], U8, "wgs")
         wes = held([P, E, N], U8, "wes")
         gate_rows = held([P, P], F32, "gate_rows")
-        a_planes = keep.tile([P, PACK + 1, C1], BF16, name="a_planes", tag="late", align_bytes=64)
         ident = held([P, P], F32, "ident")
-        ident_bf = held([P, P], BF16, "ident_bf")
 
         nc.gpsimd.memset(xs[:].bitcast(I32), 0)
         nc.vector.memset(wgs[:].bitcast(I32), 0)
         nc.vector.memset(gate_rows[:], 0.0)
         nc.vector.memset(wes[:].bitcast(I32), 0)
-        nc.vector.memset(a_planes[:, 0, :], 0.0)
         make_identity(nc, ident[:])
-        nc.scalar.copy(ident_bf[:], ident[:])
 
         def load_group(f):
             nc.sync.dma_start(wgw[f][:], wg_words[f][0].rearrange("p i d -> p (i d)").bitcast(I32))
@@ -80,9 +76,8 @@ def tile_moe_hie_none_kernel(
         nc.sync.dma_start(offs2_t[:], offs2)
         nc.sync.dma_start(dst_t[:], dst)
         for q in range(QUADS):
-            if q == 2:
-                nc.sync.dma_start(xw[:], x_words[0].rearrange("p t d -> p (t d)").bitcast(I32))
             nc.sync.dma_start(quad_rows(xs, q), x_scales[0][4 * q : 4 * q + 4].bitcast(I32))
+        nc.sync.dma_start(xw[:], x_words[0].rearrange("p t d -> p (t d)").bitcast(I32))
         load_group(0)
         wg_rows = wg_scales.rearrange("f s b i -> (s b) f i")
         for q in range(QUADS):
@@ -95,15 +90,17 @@ def tile_moe_hie_none_kernel(
         for first, count in ((0, 1), (1, 1), (2, 2), (4, 2), (6, 2)):
             load_experts(first, count)
 
-        def gather_tokens(first, count):
-            words = held([P, count], U32, f"xgw{first}")
+        def gather_scales(first, count):
             scales = held([P, count], U8, f"xgs{first}")
-            nc.vector.tensor_copy(words[:], xw[:].bitcast(U32).indirect(entries(offs_t, first, count)))
             nc.vector.tensor_copy(scales[:], xs[:].indirect(entries(offs_t, first, count)))
-            return [(words[:, c : c + P], scales[:, c : c + P]) for c in range(0, count, P)]
+            return [scales[:, c : c + P] for c in range(0, count, P)]
 
-        def group_layer(block, f, acc):
-            words, scales = block
+        def gather_words(first, count):
+            words = held([P, count], U32, f"xgw{first}")
+            nc.vector.tensor_copy(words[:], xw[:].bitcast(U32).indirect(entries(offs_t, first, count)))
+            return [words[:, c : c + P] for c in range(0, count, P)]
+
+        def group_rows(f, words, scales, acc):
             nc.tensor.matmul_mx(
                 out=acc[:],
                 lhsT=words.bitcast(FP8X4),
@@ -113,113 +110,117 @@ def tile_moe_hie_none_kernel(
                 start=True,
                 stop=True,
             )
-            return acc
-
-        a_pairs = held([P, 2, C1], F32, "a_pairs")
-        blocks0 = gather_tokens(0, 128) + gather_tokens(128, 128) + gather_tokens(256, 256)
-        turned = [bank(4 + u, [P, C1]) for u in range(2)]
-        for b in range(4):
-            acc = group_layer(blocks0[b], 0, bank(b, [P, H]))
             rows = ring.tile([P, H], BF16, name="rows", align_bytes=64)
             nc.scalar.copy(
                 rows[:].rearrange("m (u p e) -> m u p e", u=2, e=2),
                 acc[:].rearrange("m (p u e) -> m u p e", u=2, e=2),
             )
-            pairs = rows[:].bitcast(F32)
+            return rows[:].bitcast(F32)
+
+        def turn_pairs(pairs, b, turned):
             for u in range(2):
                 nc.tensor.transpose(turned[u][:, b * P : (b + 1) * P], pairs[:, u * P : (u + 1) * P], ident[:])
-
-        blocks1 = gather_tokens(C1, C1)
-        nc.scalar.copy(a_pairs[:, 0, :], turned[0][:])
-        nc.vector.tensor_copy(a_pairs[:, 1, :], turned[1][:])
-
-        gate_ps = bank(6, [P, P])
-        nc.tensor.transpose(gate_ps[:], gate_rows[:], ident[:])
-        gate_cols = held([P, E], F32, "gate_cols")
-        nc.scalar.copy(gate_cols[:], gate_ps[:, 0:E])
-
 
         def quantise(grouped, count, name):
             codes = held([P, count], U32, f"codes_{name}")
             scales = held([P, count], U8, f"scales_{name}")
             nc.vector.quantize_mx(out=codes[:].bitcast(FP8X4), scales=scales[:], in_=grouped[:])
-            return codes, scales
+            return [(codes[:, c : c + C2], scales[:, c : c + C2]) for c in range(0, count, C2)]
 
-        def regather_pairs(first, count):
+        a_pairs = [held([P, T], F32, f"a_pairs{u}") for u in range(2)]
+
+        def gather_woven(first, count, columns):
             grouped = held([P, PACK * count], BF16, f"grouped{first}")
             as_pairs = grouped[:].bitcast(U32).rearrange("p (m u) -> p m u", u=2)
             for u in range(2):
-                window = a_pairs[:, u, :].bitcast(U32)
+                window = a_pairs[u][:, 0:columns].bitcast(U32)
                 nc.vector.tensor_copy(as_pairs[:, :, u], window.indirect(entries(offs2_t, first, count)))
             return grouped
 
-        def regather_planes(first, count):
-            grouped = held([P, PACK * count], BF16, f"grouped{first}")
-            by_plane = grouped[:].rearrange("p (m t) -> p m t", t=PACK)
-            flat = a_planes[:].rearrange("p s c -> p (s c)")
-            for t in range(PACK):
-                window = flat[:, t * C1 : (t + 2) * C1]
-                nc.scalar.activation(by_plane[:, :, t], window.indirect(entries(offs2_t, first, count)), COPY)
-            return grouped
+        def gather_apart(first, count, columns):
+            apart = held([P, 2, count], U32, f"apart{first}")
+            for u in range(2):
+                window = a_pairs[u][:, 0:columns].bitcast(U32)
+                nc.vector.tensor_copy(apart[:, u, :], window.indirect(entries(offs2_t, first, count)))
+            return apart
 
-        def expert_rows(e, quantised, col):
+        def weave(apart, first, count, name):
+            grouped = held([P, PACK * count], BF16, f"grouped_{name}")
+            nc.scalar.copy(
+                grouped[:].bitcast(F32).rearrange("p (m u) -> p m u", u=2),
+                apart[:, :, first : first + count].bitcast(F32).rearrange("p u m -> p m u"),
+            )
+            return quantise(grouped, count, name)
+
+        def expert_rows(e, quantised, parts=1):
             codes, scales = quantised
-            acc = bank(e % 2 if e < 4 else e - 4, [P, N])
+            acc = bank(e % 4, [P, N])
             nc.tensor.matmul_mx(
                 out=acc[:],
-                lhsT=codes[:, col : col + P].bitcast(FP8X4),
-                lhsT_scale=scales[:, col : col + P],
+                lhsT=codes.bitcast(FP8X4),
+                lhsT_scale=scales,
                 rhs=wew[e].bitcast(FP8X4),
                 rhs_scale=wes[:, e, :],
                 start=True,
                 stop=True,
             )
             gated = ring.tile([P, PACK, P], F32, name="gated")
-            nc.scalar.activation(
-                gated[:], acc[:].rearrange("m (p t) -> m t p", t=PACK), COPY, scale=gate_cols[:, e : e + 1]
-            )
+            dealt = acc[:].rearrange("m (p t) -> m t p", t=PACK)
+            for t in range(0, PACK, PACK // parts):
+                some = slice(t, t + PACK // parts)
+                nc.scalar.activation(gated[:, some, :], dealt[:, some, :], COPY, scale=gate_cols[:, e : e + 1])
             return gated
 
         planes = [keep.tile([P, T], F32, name=f"plane{t}") for t in range(PACK)]
 
-        def expert_by_slots(e, quantised, col):
-            gated = expert_rows(e, quantised, col)
-            turned = bank((2, 3, 7, 6)[e], [P, PACK, P])
-            if e < 3:
-                y = held([P, PACK, P], F32, f"y{e}")
-            else:
-                y = keep.tile([P, PACK, P], F32, name="y3", tag="late", align_bytes=64)
-            for t in range(PACK):
-                nc.tensor.transpose(turned[:, t, :], gated[:, t, :], ident[:])
-            nc.scalar.copy(y[:], turned[:])
-            for t in range(PACK):
-                nc.vector.tensor_copy(planes[t][:].indirect(entries(dst_t, e * C2, C2)), y[:, t, :])
+        def scatter_expert(e, gated, numbers):
+            count = PACK // len(numbers)
+            for part, number in enumerate(numbers):
+                turned = bank(number, [P, count, P])
+                for j in range(count):
+                    nc.tensor.transpose(turned[:, j, :], gated[:, part * count + j, :], ident[:])
+                y = held([P, count, P], F32, f"y{e}_{part}")
+                nc.scalar.copy(y[:], turned[:])
+                for j in range(count):
+                    window = planes[part * count + j][:]
+                    nc.vector.tensor_copy(window.indirect(entries(dst_t, e * C2, C2)), y[:, j, :])
 
-        q0 = quantise(regather_pairs(0, C2), C2, "e0")
-        q1 = quantise(regather_pairs(C2, C2), C2, "e1")
-        q23 = quantise(regather_pairs(2 * C2, 2 * C2), 2 * C2, "e23")
-        expert_by_slots(0, q0, 0)
-        expert_by_slots(1, q1, 0)
+        gate_ps = bank(6, [P, P])
+        nc.tensor.transpose(gate_ps[:], gate_rows[:], ident[:])
+        gate_cols = held([P, E], F32, "gate_cols")
+        nc.scalar.copy(gate_cols[:], gate_ps[:, 0:E])
 
+        scales0 = gather_scales(0, C1)
+        words0 = gather_words(0, P) + gather_words(P, P) + gather_words(2 * P, 2 * P)
+        turned = [bank(4 + u, [P, C1]) for u in range(2)]
+        pairs = [group_rows(0, words0[b], scales0[b], bank(b, [P, H])) for b in range(4)]
         for b in range(4):
-            acc = group_layer(blocks1[b], 1, bank((4, 5, 0, 1)[b], [P, H]))
-            rows = ring.tile([P, H], BF16, name="rows", align_bytes=64)
-            nc.scalar.copy(
-                rows[:].rearrange("m (t p) -> m t p", t=PACK), acc[:].rearrange("m (p t) -> m t p", t=PACK)
-            )
-            turned = bank(6 + b % 2, [P, PACK, P], BF16)
-            for t in range(PACK):
-                nc.tensor.transpose(turned[:, t, :], rows[:, t * P : (t + 1) * P], ident_bf[:])
-            nc.scalar.copy(a_planes[:, 1:, b * P : (b + 1) * P], turned[:])
+            turn_pairs(pairs[b], b, turned)
+        scales1 = gather_scales(C1, C1)
+        words1 = gather_words(C1, C1)
+        nc.scalar.copy(a_pairs[0][:, 0:C1], turned[0][:])
+        nc.vector.tensor_copy(a_pairs[1][:, 0:C1], turned[1][:])
 
-        q45 = quantise(regather_planes(C1, 2 * C2), 2 * C2, "e45")
-        expert_by_slots(2, q23, 0)
-        q67 = quantise(regather_planes(C1 + 2 * C2, 2 * C2), 2 * C2, "e67")
-        expert_by_slots(3, q23, C2)
+        slots = quantise(gather_woven(0, C2, C1), C2, "e0")
+        slots = slots + quantise(gather_woven(C2, C2, C1), C2, "e1")
+        slots = slots + quantise(gather_woven(2 * C2, 2 * C2, C1), 2 * C2, "e23")
+        scatter_expert(0, expert_rows(0, slots[0], parts=2), (2, 3))
+        gated = expert_rows(1, slots[1])
+
+        turned = [bank(6 + u, [P, C1]) for u in range(2)]
+        for b in range(4):
+            turn_pairs(group_rows(1, words1[b], scales1[b], bank((4, 5, 0, 1)[b], [P, H])), b, turned)
+        for u in range(2):
+            nc.scalar.copy(a_pairs[u][:, C1:T], turned[u][:])
+        apart = gather_apart(C1, C1, T)
+        scatter_expert(1, gated, (6,))
+        slots = slots + weave(apart, 0, 2 * C2, "e45") + weave(apart, 2 * C2, 2 * C2, "e67")
+        for e in (2, 3):
+            scatter_expert(e, expert_rows(e, slots[e]), (6,))
 
         banks = [bank(4 + t, [P, C1]) for t in range(PACK)]
         for j in range(4):
-            gated = expert_rows(4 + j, (q45, q67)[j // 2], (j % 2) * C2)
+            gated = expert_rows(4 + j, slots[4 + j])
             for t in range(PACK):
                 nc.tensor.transpose(banks[t][:, j * P : (j + 1) * P], gated[:, t, :], ident[:])
         ys = []

@@ -19,7 +19,7 @@ P = 128
 PACK = 4
 QUADS = 4
 LANES = 16
-HALF = T // 2
+CHUNK = T // 4
 
 
 def tile_moe_hie_none_kernel(
@@ -34,8 +34,8 @@ def tile_moe_hie_none_kernel(
         def bank(number, shape, dtype=F32):
             return psum.tile(shape, dtype, name=f"bank{number}")
 
-        def held(shape, dtype, name):
-            return keep.tile(shape, dtype, name=name, align_bytes=64)
+        def held(shape, dtype, name, tag=None):
+            return keep.tile(shape, dtype, name=name, tag=tag or name, align_bytes=64)
 
         def entries(lst, first, count):
             return lst[:, first // LANES : (first + count) // LANES]
@@ -57,8 +57,8 @@ def tile_moe_hie_none_kernel(
 
         nc.gpsimd.memset(xs[:].bitcast(I32), 0)
         nc.vector.memset(wgs[:].bitcast(I32), 0)
-        nc.vector.memset(gate_rows[:], 0.0)
         nc.vector.memset(wes[:].bitcast(I32), 0)
+        nc.vector.memset(gate_rows[:], 0.0)
         make_identity(nc, ident[:])
 
         def load_group(f):
@@ -82,12 +82,13 @@ def tile_moe_hie_none_kernel(
         wg_rows = wg_scales.rearrange("f s b i -> (s b) f i")
         for q in range(QUADS):
             nc.sync.dma_start(quad_rows(wgs, q), wg_rows[4 * q : 4 * q + 4].bitcast(I32))
-        nc.sync.dma_start(gate_rows[0:E, :], gate[0:1, :].rearrange("r (e m) -> (r e) m", e=E))
-        load_group(1)
         we_rows = we_scales.rearrange("e s b n -> (s b) e n")
         for q in range(QUADS):
             nc.sync.dma_start(quad_rows(wes, q), we_rows[4 * q : 4 * q + 4].bitcast(I32))
-        for first, count in ((0, 1), (1, 1), (2, 2), (4, 2), (6, 2)):
+        nc.sync.dma_start(gate_rows[0:E, :], gate[0:1, :].rearrange("r (e m) -> (r e) m", e=E))
+        load_experts(0, 1)
+        load_group(1)
+        for first, count in ((1, 1), (2, 2), (4, 2), (6, 2)):
             load_experts(first, count)
 
         def gather_scales(first, count):
@@ -95,12 +96,12 @@ def tile_moe_hie_none_kernel(
             nc.vector.tensor_copy(scales[:], xs[:].indirect(entries(offs_t, first, count)))
             return [scales[:, c : c + P] for c in range(0, count, P)]
 
-        def gather_words(first, count):
-            words = held([P, count], U32, f"xgw{first}")
+        def gather_words(first, count, tag=None):
+            words = held([P, count], U32, f"xgw{first}", tag)
             nc.vector.tensor_copy(words[:], xw[:].bitcast(U32).indirect(entries(offs_t, first, count)))
             return [words[:, c : c + P] for c in range(0, count, P)]
 
-        def group_rows(f, words, scales, acc):
+        def group_rows(f, words, scales, acc, copy):
             nc.tensor.matmul_mx(
                 out=acc[:],
                 lhsT=words.bitcast(FP8X4),
@@ -111,7 +112,7 @@ def tile_moe_hie_none_kernel(
                 stop=True,
             )
             rows = ring.tile([P, H], BF16, name="rows", align_bytes=64)
-            nc.scalar.copy(
+            copy(
                 rows[:].rearrange("m (u p e) -> m u p e", u=2, e=2),
                 acc[:].rearrange("m (p u e) -> m u p e", u=2, e=2),
             )
@@ -130,31 +131,31 @@ def tile_moe_hie_none_kernel(
         a_pairs = [held([P, T], F32, f"a_pairs{u}") for u in range(2)]
 
         def gather_woven(first, count, columns):
-            grouped = held([P, PACK * count], BF16, f"grouped{first}")
+            grouped = held([P, PACK * count], BF16, f"grouped{first}", "first_gathers")
             as_pairs = grouped[:].bitcast(U32).rearrange("p (m u) -> p m u", u=2)
             for u in range(2):
                 window = a_pairs[u][:, 0:columns].bitcast(U32)
                 nc.vector.tensor_copy(as_pairs[:, :, u], window.indirect(entries(offs2_t, first, count)))
             return grouped
 
-        def gather_apart(first, count, columns):
-            apart = held([P, 2, count], U32, f"apart{first}")
+        def gather_apart(first, count, columns, tag=None):
+            apart = held([P, 2, count], U32, f"apart{first}", tag)
             for u in range(2):
                 window = a_pairs[u][:, 0:columns].bitcast(U32)
                 nc.vector.tensor_copy(apart[:, u, :], window.indirect(entries(offs2_t, first, count)))
             return apart
 
-        def weave(apart, first, count, name):
-            grouped = held([P, PACK * count], BF16, f"grouped_{name}")
+        def weave(apart, first, count, name, tag=None):
+            grouped = held([P, PACK * count], BF16, f"grouped_{name}", tag)
             nc.scalar.copy(
                 grouped[:].bitcast(F32).rearrange("p (m u) -> p m u", u=2),
                 apart[:, :, first : first + count].bitcast(F32).rearrange("p u m -> p m u"),
             )
             return quantise(grouped, count, name)
 
-        def expert_rows(e, quantised, parts=1):
+        def expert_rows(e, quantised, number, cuts=(0, PACK)):
             codes, scales = quantised
-            acc = bank(e % 4, [P, N])
+            acc = bank(number, [P, N])
             nc.tensor.matmul_mx(
                 out=acc[:],
                 lhsT=codes.bitcast(FP8X4),
@@ -164,95 +165,103 @@ def tile_moe_hie_none_kernel(
                 start=True,
                 stop=True,
             )
-            gated = ring.tile([P, PACK, P], F32, name="gated")
             dealt = acc[:].rearrange("m (p t) -> m t p", t=PACK)
-            for t in range(0, PACK, PACK // parts):
-                some = slice(t, t + PACK // parts)
-                nc.scalar.activation(gated[:, some, :], dealt[:, some, :], COPY, scale=gate_cols[:, e : e + 1])
+            gated = []
+            for first, last in zip(cuts, cuts[1:]):
+                part = held([P, last - first, P], F32, f"gated{e}_{first}")
+                nc.scalar.activation(part[:], dealt[:, first:last, :], COPY, scale=gate_cols[:, e : e + 1])
+                gated.extend(part[:, j, :] for j in range(last - first))
             return gated
 
         planes = [keep.tile([P, T], F32, name=f"plane{t}") for t in range(PACK)]
 
-        def scatter_expert(e, gated, numbers):
-            count = PACK // len(numbers)
-            for part, number in enumerate(numbers):
+        def scatter_planes(e, gated, parts):
+            for first, count, number in parts:
                 turned = bank(number, [P, count, P])
                 for j in range(count):
-                    nc.tensor.transpose(turned[:, j, :], gated[:, part * count + j, :], ident[:])
-                y = held([P, count, P], F32, f"y{e}_{part}")
+                    nc.tensor.transpose(turned[:, j, :], gated[first + j], ident[:])
+                y = held([P, count, P], F32, f"y{e}_{first}")
                 nc.scalar.copy(y[:], turned[:])
                 for j in range(count):
-                    window = planes[part * count + j][:]
+                    window = planes[first + j][:]
                     nc.vector.tensor_copy(window.indirect(entries(dst_t, e * C2, C2)), y[:, j, :])
 
-        gate_ps = bank(6, [P, P])
+        scales0 = gather_scales(0, C1)
+        words0 = gather_words(0, P) + gather_words(P, P) + gather_words(2 * P, 2 * P)
+        scales1 = gather_scales(C1, C1)
+        words1 = gather_words(C1, C1)
+        copies = (nc.scalar.copy, nc.vector.tensor_copy)
+        pairs = [group_rows(0, words0[b], scales0[b], bank(b, [P, H]), copies[b // 3]) for b in range(4)]
+        early = bank(4, [P, 2, 2 * P])
+        late = [bank(5 + u, [P, 2 * P]) for u in range(2)]
+        for b in range(2):
+            turn_pairs(pairs[b], b, [early[:, u, :] for u in range(2)])
+        for b in range(2):
+            turn_pairs(pairs[2 + b], b, late)
+        for u in range(2):
+            nc.scalar.copy(a_pairs[u][:, 0 : 2 * P], early[:, u, :])
+        for u in range(2):
+            copies[u](a_pairs[u][:, 2 * P : C1], late[u][:])
+
+        gate_ps = bank(7, [P, P])
         nc.tensor.transpose(gate_ps[:], gate_rows[:], ident[:])
         gate_cols = held([P, E], F32, "gate_cols")
         nc.scalar.copy(gate_cols[:], gate_ps[:, 0:E])
 
-        scales0 = gather_scales(0, C1)
-        words0 = gather_words(0, P) + gather_words(P, P) + gather_words(2 * P, 2 * P)
-        turned = [bank(4 + u, [P, C1]) for u in range(2)]
-        pairs = [group_rows(0, words0[b], scales0[b], bank(b, [P, H])) for b in range(4)]
-        for b in range(4):
-            turn_pairs(pairs[b], b, turned)
-        scales1 = gather_scales(C1, C1)
-        words1 = gather_words(C1, C1)
-        nc.scalar.copy(a_pairs[0][:, 0:C1], turned[0][:])
-        nc.vector.tensor_copy(a_pairs[1][:, 0:C1], turned[1][:])
-
         slots = quantise(gather_woven(0, C2, C1), C2, "e0")
         slots = slots + quantise(gather_woven(C2, C2, C1), C2, "e1")
-        slots = slots + quantise(gather_woven(2 * C2, 2 * C2, C1), 2 * C2, "e23")
-        scatter_expert(0, expert_rows(0, slots[0], parts=2), (2, 3))
-        gated = expert_rows(1, slots[1])
+        apart = gather_apart(2 * C2, 2 * C2, C1, "first_gathers")
+        scatter_planes(0, expert_rows(0, slots[0], 0, (0, 1, 2, 4)), ((0, 1, 1), (1, 1, 2), (2, 2, 3)))
+        slots = slots + weave(apart, 0, 2 * C2, "e23", tag="gated0_2")
+        scatter_planes(1, expert_rows(1, slots[1], 0), ((0, PACK, 4),))
 
-        turned = [bank(6 + u, [P, C1]) for u in range(2)]
-        for b in range(4):
-            turn_pairs(group_rows(1, words1[b], scales1[b], bank((4, 5, 0, 1)[b], [P, H])), b, turned)
-        for u in range(2):
-            nc.scalar.copy(a_pairs[u][:, C1:T], turned[u][:])
+        pairs = [group_rows(1, words1[b], scales1[b], bank((5, 6, 1, 0)[b], [P, H]), nc.scalar.copy) for b in range(4)]
+        for h in range(2):
+            turned = bank(2 + h, [P, 2, 2 * P])
+            for b in range(2):
+                turn_pairs(pairs[2 * h + b], b, [turned[:, u, :] for u in range(2)])
+            for u in range(2):
+                nc.scalar.copy(a_pairs[u][:, C1 + 2 * P * h : C1 + 2 * P * (h + 1)], turned[:, u, :])
         apart = gather_apart(C1, C1, T)
-        scatter_expert(1, gated, (6,))
-        slots = slots + weave(apart, 0, 2 * C2, "e45") + weave(apart, 2 * C2, 2 * C2, "e67")
-        for e in (2, 3):
-            scatter_expert(e, expert_rows(e, slots[e]), (6,))
+        gated = expert_rows(2, slots[2], 3, (0, 2, 4))
+        scatter_planes(2, gated, ((0, 2, 2),))
+        slots = slots + weave(apart, 0, C1, "group1", tag="gated2_0")
+        scatter_planes(2, gated, ((2, 2, 2),))
+        scatter_planes(3, expert_rows(3, slots[3], 3), ((0, PACK, 2),))
 
-        banks = [bank(4 + t, [P, C1]) for t in range(PACK)]
-        for j in range(4):
-            gated = expert_rows(4 + j, slots[4 + j])
-            for t in range(PACK):
-                nc.tensor.transpose(banks[t][:, j * P : (j + 1) * P], gated[:, t, :], ident[:])
+        gated = [expert_rows(4 + j, slots[4 + j], (0, 1, 3, 2)[j]) for j in range(4)]
         ys = []
         for t in range(PACK):
-            y = held([P, C1], F32, f"y1_{t}")
-            nc.scalar.copy(y[:], banks[t][:])
+            turned = bank(4 + t, [P, C1])
+            for j in range(4):
+                nc.tensor.transpose(turned[:, j * P : (j + 1) * P], gated[j][t], ident[:])
+            y = held([P, C1], F32, f"y_group1_{t}")
+            nc.scalar.copy(y[:], turned[:])
             ys.append(y)
 
-        rounded = [held([P, HALF, PACK], BF16, f"rounded{h}") for h in range(2)]
-        last_pair = held([P, 2, HALF], BF16, "last_pair")
+        chunks = [slice(c, c + CHUNK) for c in range(0, T, CHUNK)]
+        rounded = [held([P, CHUNK, PACK], BF16, f"rounded{c}") for c in range(4)]
+        last_pair = [held([P, 2, CHUNK], BF16, f"last_pair{c}") for c in range(2)]
         out_rows = out_0.rearrange("(p t) c -> p t c", t=PACK)
         for t in range(PACK):
             nc.vector.tensor_copy(planes[t][:].indirect(entries(dst_t, C1, C1)), ys[t][:])
             nc.sync.dma_start(out_rows[:, t, :], planes[t][:])
-            if t < 2:
-                nc.scalar.copy(rounded[0][:, :, t], planes[t][:, 0:HALF])
-            elif t == 2:
-                nc.scalar.copy(last_pair[:, 0, :], planes[t][:, 0:HALF])
-            else:
-                nc.vector.tensor_copy(last_pair[:, 1, :], planes[t][:, 0:HALF])
-                nc.vector.tensor_copy(rounded[0][:, :, 2:4], last_pair[:].rearrange("p e m -> p m e"))
-            nc.scalar.copy(rounded[1][:, :, t], planes[t][:, HALF:T])
+            for c, cols in enumerate(chunks):
+                if t < 2 or c >= 2:
+                    nc.scalar.copy(rounded[c][:, :, t], planes[t][:, cols])
+                else:
+                    copies[t - 2](last_pair[c][:, t - 2, :], planes[t][:, cols])
+        for c in range(2):
+            nc.vector.tensor_copy(rounded[c][:, :, 2:4], last_pair[c][:].rearrange("p e m -> p m e"))
 
         out_scales = held([P, T], U8, "out_scales")
         out_words = out_1[0].rearrange("p t d -> p (t d)").bitcast(I32)
-        for h in range(2):
-            cols = slice(h * HALF, (h + 1) * HALF)
-            codes = held([P, HALF], U32, f"out_codes{h}")
+        for c, cols in enumerate(chunks):
+            codes = held([P, CHUNK], U32, f"out_codes{c}")
             nc.vector.quantize_mx(
                 out=codes[:].bitcast(FP8X4),
                 scales=out_scales[:, cols],
-                in_=rounded[h][:].rearrange("p m t -> p (m t)"),
+                in_=rounded[c][:].rearrange("p m t -> p (m t)"),
             )
             nc.sync.dma_start(out_words[:, cols], codes[:].bitcast(I32))
         for q in range(QUADS):

@@ -131,7 +131,7 @@ def tile_moe_hie_none_kernel(
         a_pairs = [held([P, T], F32, f"a_pairs{u}") for u in range(2)]
 
         def gather_woven(first, count, columns):
-            grouped = held([P, PACK * count], BF16, f"grouped{first}", "first_gathers")
+            grouped = held([P, PACK * count], BF16, f"grouped{first}")
             as_pairs = grouped[:].bitcast(U32).rearrange("p (m u) -> p m u", u=2)
             for u in range(2):
                 window = a_pairs[u][:, 0:columns].bitcast(U32)
@@ -210,7 +210,7 @@ def tile_moe_hie_none_kernel(
 
         slots = quantise(gather_woven(0, C2, C1), C2, "e0")
         slots = slots + quantise(gather_woven(C2, C2, C1), C2, "e1")
-        apart = gather_apart(2 * C2, 2 * C2, C1, "first_gathers")
+        apart = gather_apart(2 * C2, 2 * C2, C1, "grouped0")
         scatter_planes(0, expert_rows(0, slots[0], 0, (0, 1, 2, 4)), ((0, 1, 1), (1, 1, 2), (2, 2, 3)))
         slots = slots + weave(apart, 0, 2 * C2, "e23", tag="gated0_2")
         scatter_planes(1, expert_rows(1, slots[1], 0), ((0, PACK, 4),))
@@ -223,9 +223,11 @@ def tile_moe_hie_none_kernel(
             for u in range(2):
                 nc.scalar.copy(a_pairs[u][:, C1 + 2 * P * h : C1 + 2 * P * (h + 1)], turned[:, u, :])
         apart = gather_apart(C1, C1, T)
-        gated = expert_rows(2, slots[2], 3, (0, 2, 4))
-        scatter_planes(2, gated, ((0, 2, 2),))
-        slots = slots + weave(apart, 0, C1, "group1", tag="gated2_0")
+        gated = expert_rows(2, slots[2], 3, (0, 1, 2, 4))
+        scatter_planes(2, gated, ((0, 1, 2),))
+        slots = slots + weave(apart, 0, 2 * C2, "e45", tag="gated2_0")
+        scatter_planes(2, gated, ((1, 1, 2),))
+        slots = slots + weave(apart, 2 * C2, 2 * C2, "e67", tag="gated2_1")
         scatter_planes(2, gated, ((2, 2, 2),))
         scatter_planes(3, expert_rows(3, slots[3], 3), ((0, PACK, 2),))
 

@@ -17,9 +17,13 @@ COPY = mybir.ActivationFunctionType.Copy
 
 P = 128
 PACK = 4
+PAIRS = 2
 QUADS = 4
 LANES = 16
+BLOCKS = C1 // P
+PER_GROUP = E // G
 CHUNK = T // 4
+VECTOR_CHUNKS = 2
 
 
 def tile_moe_hie_none_kernel(
@@ -28,19 +32,19 @@ def tile_moe_hie_none_kernel(
     nc = tc.nc
     with ExitStack() as ctx:
         keep = ctx.enter_context(tc.tile_pool(name="keep", bufs=1))
-        ring = ctx.enter_context(tc.tile_pool(name="ring", bufs=4))
+        ring = ctx.enter_context(tc.tile_pool(name="ring", bufs=BLOCKS))
         psum = ctx.enter_context(tc.psum_pool(name="psum", bufs=1))
 
-        def bank(number, shape, dtype=F32):
-            return psum.tile(shape, dtype, name=f"bank{number}")
+        def bank(number, shape):
+            return psum.tile(shape, F32, name=f"bank{number}")
 
-        def held(shape, dtype, name, tag=None):
-            return keep.tile(shape, dtype, name=name, tag=tag or name, align_bytes=64)
+        def held(shape, dtype, name, slot_of=None):
+            return keep.tile(shape, dtype, name=name, tag=slot_of or name, align_bytes=64)
 
-        def entries(lst, first, count):
-            return lst[:, first // LANES : (first + count) // LANES]
+        def entries(list_tile, first, count):
+            return list_tile[:, first // LANES : (first + count) // LANES]
 
-        def quad_rows(plane, q):
+        def scale_rows(plane, q):
             return plane[32 * q : 32 * q + 4].bitcast(I32)
 
         offs_t = keep.tile([P, T // LANES], U16, name="offs_t")
@@ -76,28 +80,29 @@ def tile_moe_hie_none_kernel(
         nc.sync.dma_start(offs2_t[:], offs2)
         nc.sync.dma_start(dst_t[:], dst)
         for q in range(QUADS):
-            nc.sync.dma_start(quad_rows(xs, q), x_scales[0][4 * q : 4 * q + 4].bitcast(I32))
+            nc.sync.dma_start(scale_rows(xs, q), x_scales[0][4 * q : 4 * q + 4].bitcast(I32))
         nc.sync.dma_start(xw[:], x_words[0].rearrange("p t d -> p (t d)").bitcast(I32))
         load_group(0)
         wg_rows = wg_scales.rearrange("f s b i -> (s b) f i")
         for q in range(QUADS):
-            nc.sync.dma_start(quad_rows(wgs, q), wg_rows[4 * q : 4 * q + 4].bitcast(I32))
+            nc.sync.dma_start(scale_rows(wgs, q), wg_rows[4 * q : 4 * q + 4].bitcast(I32))
         we_rows = we_scales.rearrange("e s b n -> (s b) e n")
         for q in range(QUADS):
-            nc.sync.dma_start(quad_rows(wes, q), we_rows[4 * q : 4 * q + 4].bitcast(I32))
+            nc.sync.dma_start(scale_rows(wes, q), we_rows[4 * q : 4 * q + 4].bitcast(I32))
         nc.sync.dma_start(gate_rows[0:E, :], gate[0:1, :].rearrange("r (e m) -> (r e) m", e=E))
         load_experts(0, 1)
         load_group(1)
-        for first, count in ((1, 1), (2, 2), (4, 2), (6, 2)):
-            load_experts(first, count)
+        load_experts(1, 1)
+        for first in range(2, E, 2):
+            load_experts(first, 2)
 
         def gather_scales(first, count):
             scales = held([P, count], U8, f"xgs{first}")
             nc.vector.tensor_copy(scales[:], xs[:].indirect(entries(offs_t, first, count)))
             return [scales[:, c : c + P] for c in range(0, count, P)]
 
-        def gather_words(first, count, tag=None):
-            words = held([P, count], U32, f"xgw{first}", tag)
+        def gather_words(first, count):
+            words = held([P, count], U32, f"xgw{first}")
             nc.vector.tensor_copy(words[:], xw[:].bitcast(U32).indirect(entries(offs_t, first, count)))
             return [words[:, c : c + P] for c in range(0, count, P)]
 
@@ -113,13 +118,13 @@ def tile_moe_hie_none_kernel(
             )
             rows = ring.tile([P, H], BF16, name="rows", align_bytes=64)
             copy(
-                rows[:].rearrange("m (u p e) -> m u p e", u=2, e=2),
-                acc[:].rearrange("m (p u e) -> m u p e", u=2, e=2),
+                rows[:].rearrange("m (u p e) -> m u p e", u=PAIRS, e=2),
+                acc[:].rearrange("m (p u e) -> m u p e", u=PAIRS, e=2),
             )
             return rows[:].bitcast(F32)
 
         def turn_pairs(pairs, b, turned):
-            for u in range(2):
+            for u in range(PAIRS):
                 nc.tensor.transpose(turned[u][:, b * P : (b + 1) * P], pairs[:, u * P : (u + 1) * P], ident[:])
 
         def quantise(grouped, count, name):
@@ -128,34 +133,34 @@ def tile_moe_hie_none_kernel(
             nc.vector.quantize_mx(out=codes[:].bitcast(FP8X4), scales=scales[:], in_=grouped[:])
             return [(codes[:, c : c + C2], scales[:, c : c + C2]) for c in range(0, count, C2)]
 
-        a_pairs = [held([P, T], F32, f"a_pairs{u}") for u in range(2)]
+        a_pairs = [held([P, T], F32, f"a_pairs{u}") for u in range(PAIRS)]
 
-        def gather_woven(first, count, columns):
-            grouped = held([P, PACK * count], BF16, f"grouped{first}")
-            as_pairs = grouped[:].bitcast(U32).rearrange("p (m u) -> p m u", u=2)
-            for u in range(2):
-                window = a_pairs[u][:, 0:columns].bitcast(U32)
-                nc.vector.tensor_copy(as_pairs[:, :, u], window.indirect(entries(offs2_t, first, count)))
-            return grouped
+        def gather_woven(e):
+            grouped = held([P, PACK * C2], BF16, f"grouped{e}")
+            as_pairs = grouped[:].bitcast(U32).rearrange("p (m u) -> p m u", u=PAIRS)
+            for u in range(PAIRS):
+                window = a_pairs[u][:, 0:C1].bitcast(U32)
+                nc.vector.tensor_copy(as_pairs[:, :, u], window.indirect(entries(offs2_t, e * C2, C2)))
+            return quantise(grouped, C2, f"e{e}")
 
-        def gather_apart(first, count, columns, tag=None):
-            apart = held([P, 2, count], U32, f"apart{first}", tag)
-            for u in range(2):
+        def gather_apart(first, count, columns, slot_of=None):
+            apart = held([P, PAIRS, count], U32, f"apart{first}", slot_of)
+            for u in range(PAIRS):
                 window = a_pairs[u][:, 0:columns].bitcast(U32)
                 nc.vector.tensor_copy(apart[:, u, :], window.indirect(entries(offs2_t, first, count)))
             return apart
 
-        def weave(apart, first, count, name, tag=None):
-            grouped = held([P, PACK * count], BF16, f"grouped_{name}", tag)
+        def weave(apart, count, name, slot_of):
+            grouped = held([P, PACK * count], BF16, f"grouped_{name}", slot_of)
             nc.scalar.copy(
-                grouped[:].bitcast(F32).rearrange("p (m u) -> p m u", u=2),
-                apart[:, :, first : first + count].bitcast(F32).rearrange("p u m -> p m u"),
+                grouped[:].bitcast(F32).rearrange("p (m u) -> p m u", u=PAIRS),
+                apart[:].bitcast(F32).rearrange("p u m -> p m u"),
             )
             return quantise(grouped, count, name)
 
-        def expert_rows(e, quantised, number, cuts=(0, PACK)):
+        def expert_rows(e, quantised, acc_bank, cuts=(0, PACK)):
             codes, scales = quantised
-            acc = bank(number, [P, N])
+            acc = bank(acc_bank, [P, N])
             nc.tensor.matmul_mx(
                 out=acc[:],
                 lhsT=codes.bitcast(FP8X4),
@@ -175,32 +180,32 @@ def tile_moe_hie_none_kernel(
 
         planes = [keep.tile([P, T], F32, name=f"plane{t}") for t in range(PACK)]
 
-        def scatter_planes(e, gated, parts):
-            for first, count, number in parts:
-                turned = bank(number, [P, count, P])
-                for j in range(count):
-                    nc.tensor.transpose(turned[:, j, :], gated[first + j], ident[:])
-                y = held([P, count, P], F32, f"y{e}_{first}")
-                nc.scalar.copy(y[:], turned[:])
-                for j in range(count):
-                    window = planes[first + j][:]
-                    nc.vector.tensor_copy(window.indirect(entries(dst_t, e * C2, C2)), y[:, j, :])
+        def scatter_planes(e, gated, first, last, turn_bank):
+            turned = bank(turn_bank, [P, last - first, P])
+            for t in range(first, last):
+                nc.tensor.transpose(turned[:, t - first, :], gated[t], ident[:])
+            y = held([P, last - first, P], F32, f"y{e}_{first}")
+            nc.scalar.copy(y[:], turned[:])
+            for t in range(first, last):
+                nc.vector.tensor_copy(planes[t][:].indirect(entries(dst_t, e * C2, C2)), y[:, t - first, :])
 
         scales0 = gather_scales(0, C1)
         words0 = gather_words(0, P) + gather_words(P, P) + gather_words(2 * P, 2 * P)
         scales1 = gather_scales(C1, C1)
         words1 = gather_words(C1, C1)
         copies = (nc.scalar.copy, nc.vector.tensor_copy)
-        pairs = [group_rows(0, words0[b], scales0[b], bank(b, [P, H]), copies[b // 3]) for b in range(4)]
-        early = bank(4, [P, 2, 2 * P])
-        late = [bank(5 + u, [P, 2 * P]) for u in range(2)]
+        pairs = [
+            group_rows(0, words0[b], scales0[b], bank(b, [P, H]), copies[b == BLOCKS - 1]) for b in range(BLOCKS)
+        ]
+        early = bank(4, [P, PAIRS, 2 * P])
+        late = [bank(5 + u, [P, 2 * P]) for u in range(PAIRS)]
         for b in range(2):
-            turn_pairs(pairs[b], b, [early[:, u, :] for u in range(2)])
+            turn_pairs(pairs[b], b, [early[:, u, :] for u in range(PAIRS)])
         for b in range(2):
             turn_pairs(pairs[2 + b], b, late)
-        for u in range(2):
+        for u in range(PAIRS):
             nc.scalar.copy(a_pairs[u][:, 0 : 2 * P], early[:, u, :])
-        for u in range(2):
+        for u in range(PAIRS):
             copies[u](a_pairs[u][:, 2 * P : C1], late[u][:])
 
         gate_ps = bank(7, [P, P])
@@ -208,53 +213,58 @@ def tile_moe_hie_none_kernel(
         gate_cols = held([P, E], F32, "gate_cols")
         nc.scalar.copy(gate_cols[:], gate_ps[:, 0:E])
 
-        slots = quantise(gather_woven(0, C2, C1), C2, "e0")
-        slots = slots + quantise(gather_woven(C2, C2, C1), C2, "e1")
+        slots = gather_woven(0)
+        slots = slots + gather_woven(1)
         apart = gather_apart(2 * C2, 2 * C2, C1, "grouped0")
-        scatter_planes(0, expert_rows(0, slots[0], 0, (0, 1, 2, 4)), ((0, 1, 1), (1, 1, 2), (2, 2, 3)))
-        slots = slots + weave(apart, 0, 2 * C2, "e23", tag="gated0_2")
-        scatter_planes(1, expert_rows(1, slots[1], 0), ((0, PACK, 4),))
+        cuts = (0, 1, 2, PACK)
+        gated = expert_rows(0, slots[0], 0, cuts)
+        for run, (first, last) in enumerate(zip(cuts, cuts[1:])):
+            scatter_planes(0, gated, first, last, 1 + run)
+        slots = slots + weave(apart, 2 * C2, "e23", "gated0_2")
+        scatter_planes(1, expert_rows(1, slots[1], 0), 0, PACK, 4)
 
-        pairs = [group_rows(1, words1[b], scales1[b], bank((5, 6, 1, 0)[b], [P, H]), nc.scalar.copy) for b in range(4)]
+        pairs = [
+            group_rows(1, words1[b], scales1[b], bank(number, [P, H]), nc.scalar.copy)
+            for b, number in enumerate((5, 6, 1, 0))
+        ]
         for h in range(2):
-            turned = bank(2 + h, [P, 2, 2 * P])
+            turned = bank(2 + h, [P, PAIRS, 2 * P])
             for b in range(2):
-                turn_pairs(pairs[2 * h + b], b, [turned[:, u, :] for u in range(2)])
-            for u in range(2):
+                turn_pairs(pairs[2 * h + b], b, [turned[:, u, :] for u in range(PAIRS)])
+            for u in range(PAIRS):
                 nc.scalar.copy(a_pairs[u][:, C1 + 2 * P * h : C1 + 2 * P * (h + 1)], turned[:, u, :])
-        apart = gather_apart(C1, C1, T)
-        gated = expert_rows(2, slots[2], 3, (0, 1, 2, 4))
-        scatter_planes(2, gated, ((0, 1, 2),))
-        slots = slots + weave(apart, 0, 2 * C2, "e45", tag="gated2_0")
-        scatter_planes(2, gated, ((1, 1, 2),))
-        slots = slots + weave(apart, 2 * C2, 2 * C2, "e67", tag="gated2_1")
-        scatter_planes(2, gated, ((2, 2, 2),))
-        scatter_planes(3, expert_rows(3, slots[3], 3), ((0, PACK, 2),))
 
-        gated = [expert_rows(4 + j, slots[4 + j], (0, 1, 3, 2)[j]) for j in range(4)]
+        apart = gather_apart(C1, C1, T)
+        gated = expert_rows(2, slots[2], 3, (0, 2, PACK))
+        scatter_planes(2, gated, 0, 2, 2)
+        slots = slots + weave(apart, C1, "group1", "gated2_0")
+        scatter_planes(2, gated, 2, PACK, 2)
+        scatter_planes(3, expert_rows(3, slots[3], 0), 0, PACK, 2)
+
+        gated = [expert_rows(PER_GROUP + j, slots[PER_GROUP + j], (0, 1, 3, 0)[j]) for j in range(PER_GROUP)]
         ys = []
         for t in range(PACK):
             turned = bank(4 + t, [P, C1])
-            for j in range(4):
-                nc.tensor.transpose(turned[:, j * P : (j + 1) * P], gated[j][t], ident[:])
+            for j in range(PER_GROUP):
+                nc.tensor.transpose(turned[:, j * C2 : (j + 1) * C2], gated[j][t], ident[:])
             y = held([P, C1], F32, f"y_group1_{t}")
             nc.scalar.copy(y[:], turned[:])
             ys.append(y)
 
         chunks = [slice(c, c + CHUNK) for c in range(0, T, CHUNK)]
-        rounded = [held([P, CHUNK, PACK], BF16, f"rounded{c}") for c in range(4)]
-        last_pair = [held([P, 2, CHUNK], BF16, f"last_pair{c}") for c in range(2)]
+        rounded = [held([P, CHUNK, PACK], BF16, f"rounded{c}") for c in range(len(chunks))]
+        last_pair = [held([P, 2, CHUNK], BF16, f"last_pair{c}") for c in range(VECTOR_CHUNKS)]
         out_rows = out_0.rearrange("(p t) c -> p t c", t=PACK)
         for t in range(PACK):
             nc.vector.tensor_copy(planes[t][:].indirect(entries(dst_t, C1, C1)), ys[t][:])
             nc.sync.dma_start(out_rows[:, t, :], planes[t][:])
             for c, cols in enumerate(chunks):
-                if t < 2 or c >= 2:
+                if t < 2 or c >= VECTOR_CHUNKS:
                     nc.scalar.copy(rounded[c][:, :, t], planes[t][:, cols])
                 else:
-                    copies[t - 2](last_pair[c][:, t - 2, :], planes[t][:, cols])
-        for c in range(2):
-            nc.vector.tensor_copy(rounded[c][:, :, 2:4], last_pair[c][:].rearrange("p e m -> p m e"))
+                    copies[t == PACK - 1](last_pair[c][:, t - 2, :], planes[t][:, cols])
+        for c in range(VECTOR_CHUNKS):
+            nc.vector.tensor_copy(rounded[c][:, :, 2:PACK], last_pair[c][:].rearrange("p e m -> p m e"))
 
         out_scales = held([P, T], U8, "out_scales")
         out_words = out_1[0].rearrange("p t d -> p (t d)").bitcast(I32)
@@ -268,4 +278,4 @@ def tile_moe_hie_none_kernel(
             nc.sync.dma_start(out_words[:, cols], codes[:].bitcast(I32))
         for q in range(QUADS):
             queue = nc.sync if q % 2 else nc.scalar
-            queue.dma_start(out_2[0][4 * q : 4 * q + 4].bitcast(I32), quad_rows(out_scales, q))
+            queue.dma_start(out_2[0][4 * q : 4 * q + 4].bitcast(I32), scale_rows(out_scales, q))

from contextlib import ExitStack

import concourse.mybir as mybir
from concourse.masks import make_identity

K, T, G, C1, E, C2, H, N = 512, 1024, 2, 512, 8, 128, 512, 512
FLOPS = 2 * K * H * T + 2 * H * N * T

F32 = mybir.dt.float32
BF16 = mybir.dt.bfloat16
I32 = mybir.dt.int32
U32 = mybir.dt.uint32
U16 = mybir.dt.uint16
U8 = mybir.dt.uint8
FP8X4 = mybir.dt.float8_e4m3fn_x4
COPY = mybir.ActivationFunctionType.Copy

P = 128
PACK = 4
PAIRS = 2
QUADS = 4
LANES = 16
BLOCKS = C1 // P
PER_GROUP = E // G
CHUNK = T // 4
VECTOR_CHUNKS = 2


def tile_moe_hie_none_kernel(
    tc, x_words, x_scales, wg_words, wg_scales, we_words, we_scales, gate, offs, offs2, dst, out_0, out_1, out_2
):
    nc = tc.nc
    with ExitStack() as ctx:
        keep = ctx.enter_context(tc.tile_pool(name="keep", bufs=1))
        ring = ctx.enter_context(tc.tile_pool(name="ring", bufs=BLOCKS))
        psum = ctx.enter_context(tc.psum_pool(name="psum", bufs=1))

        def bank(number, shape):
            return psum.tile(shape, F32, name=f"bank{number}")

        def held(shape, dtype, name, slot_of=None):
            return keep.tile(shape, dtype, name=name, tag=slot_of or name, align_bytes=64)

        def entries(list_tile, first, count):
            return list_tile[:, first // LANES : (first + count) // LANES]

        def scale_rows(plane, q):
            return plane[32 * q : 32 * q + 4].bitcast(I32)

        offs_t = keep.tile([P, T // LANES], U16, name="offs_t")
        offs2_t = keep.tile([P, T // LANES], U16, name="offs2_t")
        dst_t = keep.tile([P, T // LANES], U16, name="dst_t")

        xw = held([P, T], I32, "xw")
        xs = held([P, T], U8, "xs")
        wgw = [held([P, H], I32, f"wgw{f}") for f in range(G)]
        wgs = held([P, G, H], U8, "wgs")
        wes = held([P, E, N], U8, "wes")
        gate_rows = held([P, P], F32, "gate_rows")
        ident = held([P, P], F32, "ident")

        nc.gpsimd.memset(xs[:].bitcast(I32), 0)
        nc.vector.memset(wgs[:].bitcast(I32), 0)
        nc.vector.memset(wes[:].bitcast(I32), 0)
        nc.vector.memset(gate_rows[:], 0.0)
        make_identity(nc, ident[:])

        def load_group(f):
            nc.sync.dma_start(wgw[f][:], wg_words[f][0].rearrange("p i d -> p (i d)").bitcast(I32))

        we_cols = we_words.rearrange("e s p n d -> (s p) e (n d)").bitcast(I32)
        wew = []

        def load_experts(first, count):
            part = held([P, count, N], I32, f"wew{first}")
            nc.sync.dma_start(part[:], we_cols[:, first : first + count, :])
            wew.extend(part[:, j, :] for j in range(count))

        nc.sync.dma_start(offs_t[:], offs)
        nc.sync.dma_start(offs2_t[:], offs2)
        nc.sync.dma_start(dst_t[:], dst)
        for q in range(QUADS):
            nc.sync.dma_start(scale_rows(xs, q), x_scales[0][4 * q : 4 * q + 4].bitcast(I32))
        nc.sync.dma_start(xw[:], x_words[0].rearrange("p t d -> p (t d)").bitcast(I32))
        load_group(0)
        wg_rows = wg_scales.rearrange("f s b i -> (s b) f i")
        for q in range(QUADS):
            nc.sync.dma_start(scale_rows(wgs, q), wg_rows[4 * q : 4 * q + 4].bitcast(I32))
        we_rows = we_scales.rearrange("e s b n -> (s b) e n")
        for q in range(QUADS):
            nc.sync.dma_start(scale_rows(wes, q), we_rows[4 * q : 4 * q + 4].bitcast(I32))
        nc.sync.dma_start(gate_rows[0:E, :], gate[0:1, :].rearrange("r (e m) -> (r e) m", e=E))
        load_experts(0, 1)
        load_group(1)
        load_experts(1, 1)
        for first in range(2, E, 2):
            load_experts(first, 2)

        def gather_scales(first, count):
            scales = held([P, count], U8, f"xgs{first}")
            nc.vector.tensor_copy(scales[:], xs[:].indirect(entries(offs_t, first, count)))
            return [scales[:, c : c + P] for c in range(0, count, P)]

        def gather_words(first, count):
            words = held([P, count], U32, f"xgw{first}")
            nc.vector.tensor_copy(words[:], xw[:].bitcast(U32).indirect(entries(offs_t, first, count)))
            return [words[:, c : c + P] for c in range(0, count, P)]

        def group_rows(f, words, scales, acc, copy):
            nc.tensor.matmul_mx(
                out=acc[:],
                lhsT=words.bitcast(FP8X4),
                lhsT_scale=scales,
                rhs=wgw[f][:].bitcast(FP8X4),
                rhs_scale=wgs[:, f, :],
                start=True,
                stop=True,
            )
            rows = ring.tile([P, H], BF16, name="rows", align_bytes=64)
            copy(
                rows[:].rearrange("m (u p e) -> m u p e", u=PAIRS, e=2),
                acc[:].rearrange("m (p u e) -> m u p e", u=PAIRS, e=2),
            )
            return rows[:].bitcast(F32)

        def turn_pairs(pairs, b, turned):
            for u in range(PAIRS):
                nc.tensor.transpose(turned[u][:, b * P : (b + 1) * P], pairs[:, u * P : (u + 1) * P], ident[:])

        def quantise(grouped, count, name):
            codes = held([P, count], U32, f"codes_{name}")
            scales = held([P, count], U8, f"scales_{name}")
            nc.vector.quantize_mx(out=codes[:].bitcast(FP8X4), scales=scales[:], in_=grouped[:])
            return [(codes[:, c : c + C2], scales[:, c : c + C2]) for c in range(0, count, C2)]

        a_pairs = [held([P, T], F32, f"a_pairs{u}") for u in range(PAIRS)]

        def gather_woven(e):
            grouped = held([P, PACK * C2], BF16, f"grouped{e}")
            as_pairs = grouped[:].bitcast(U32).rearrange("p (m u) -> p m u", u=PAIRS)
            for u in range(PAIRS):
                window = a_pairs[u][:, 0:C1].bitcast(U32)
                nc.vector.tensor_copy(as_pairs[:, :, u], window.indirect(entries(offs2_t, e * C2, C2)))
            return quantise(grouped, C2, f"e{e}")

        def gather_apart(first, count, columns, slot_of=None):
            apart = held([P, PAIRS, count], U32, f"apart{first}", slot_of)
            for u in range(PAIRS):
                window = a_pairs[u][:, 0:columns].bitcast(U32)
                nc.vector.tensor_copy(apart[:, u, :], window.indirect(entries(offs2_t, first, count)))
            return apart

        def weave(apart, count, name, slot_of):
            grouped = held([P, PACK * count], BF16, f"grouped_{name}", slot_of)
            nc.scalar.copy(
                grouped[:].bitcast(F32).rearrange("p (m u) -> p m u", u=PAIRS),
                apart[:].bitcast(F32).rearrange("p u m -> p m u"),
            )
            return quantise(grouped, count, name)

        def expert_rows(e, quantised, acc_bank, cuts=(0, PACK)):
            codes, scales = quantised
            acc = bank(acc_bank, [P, N])
            nc.tensor.matmul_mx(
                out=acc[:],
                lhsT=codes.bitcast(FP8X4),
                lhsT_scale=scales,
                rhs=wew[e].bitcast(FP8X4),
                rhs_scale=wes[:, e, :],
                start=True,
                stop=True,
            )
            dealt = acc[:].rearrange("m (p t) -> m t p", t=PACK)
            gated = []
            for first, last in zip(cuts, cuts[1:]):
                part = held([P, last - first, P], F32, f"gated{e}_{first}")
                nc.scalar.activation(part[:], dealt[:, first:last, :], COPY, scale=gate_cols[:, e : e + 1])
                gated.extend(part[:, j, :] for j in range(last - first))
            return gated

        planes = [keep.tile([P, T], F32, name=f"plane{t}") for t in range(PACK)]

        def scatter_planes(e, gated, first, last, turn_bank):
            turned = bank(turn_bank, [P, last - first, P])
            for t in range(first, last):
                nc.tensor.transpose(turned[:, t - first, :], gated[t], ident[:])
            y = held([P, last - first, P], F32, f"y{e}_{first}")
            nc.scalar.copy(y[:], turned[:])
            for t in range(first, last):
                nc.vector.tensor_copy(planes[t][:].indirect(entries(dst_t, e * C2, C2)), y[:, t - first, :])

        scales0 = gather_scales(0, C1)
        words0 = gather_words(0, P) + gather_words(P, P) + gather_words(2 * P, 2 * P)
        scales1 = gather_scales(C1, C1)
        words1 = gather_words(C1, C1)
        copies = (nc.scalar.copy, nc.vector.tensor_copy)
        pairs = [
            group_rows(0, words0[b], scales0[b], bank(b, [P, H]), copies[b == BLOCKS - 1]) for b in range(BLOCKS)
        ]
        early = bank(4, [P, PAIRS, 2 * P])
        late = [bank(5 + u, [P, 2 * P]) for u in range(PAIRS)]
        for b in range(2):
            turn_pairs(pairs[b], b, [early[:, u, :] for u in range(PAIRS)])
        for b in range(2):
            turn_pairs(pairs[2 + b], b, late)
        for u in range(PAIRS):
            nc.scalar.copy(a_pairs[u][:, 0 : 2 * P], early[:, u, :])
        for u in range(PAIRS):
            copies[u](a_pairs[u][:, 2 * P : C1], late[u][:])

        gate_ps = bank(7, [P, P])
        nc.tensor.transpose(gate_ps[:], gate_rows[:], ident[:])
        gate_cols = held([P, E], F32, "gate_cols")
        nc.scalar.copy(gate_cols[:], gate_ps[:, 0:E])

        slots = gather_woven(0)
        slots = slots + gather_woven(1)
        apart = gather_apart(2 * C2, 2 * C2, C1, "grouped0")
        cuts = (0, 1, 2, PACK)
        gated = expert_rows(0, slots[0], 0, cuts)
        for run, (first, last) in enumerate(zip(cuts, cuts[1:])):
            scatter_planes(0, gated, first, last, 1 + run)
        slots = slots + weave(apart, 2 * C2, "e23", "gated0_2")
        scatter_planes(1, expert_rows(1, slots[1], 0), 0, PACK, 4)

        pairs = [
            group_rows(1, words1[b], scales1[b], bank(number, [P, H]), nc.scalar.copy)
            for b, number in enumerate((5, 6, 1, 0))
        ]
        for h in range(2):
            turned = bank(2 + h, [P, PAIRS, 2 * P])
            for b in range(2):
                turn_pairs(pairs[2 * h + b], b, [turned[:, u, :] for u in range(PAIRS)])
            for u in range(PAIRS):
                nc.scalar.copy(a_pairs[u][:, C1 + 2 * P * h : C1 + 2 * P * (h + 1)], turned[:, u, :])

        apart = gather_apart(C1, C1, T)
        gated = expert_rows(2, slots[2], 3, (0, 2, PACK))
        scatter_planes(2, gated, 0, 2, 2)
        slots = slots + weave(apart, C1, "group1", "gated2_0")
        scatter_planes(2, gated, 2, PACK, 2)
        scatter_planes(3, expert_rows(3, slots[3], 0), 0, PACK, 2)

        gated = [expert_rows(PER_GROUP + j, slots[PER_GROUP + j], (0, 1, 3, 0)[j]) for j in range(PER_GROUP)]
        ys = []
        for t in range(PACK):
            turned = bank(4 + t, [P, C1])
            for j in range(PER_GROUP):
                nc.tensor.transpose(turned[:, j * C2 : (j + 1) * C2], gated[j][t], ident[:])
            y = held([P, C1], F32, f"y_group1_{t}")
            nc.scalar.copy(y[:], turned[:])
            ys.append(y)

        chunks = [slice(c, c + CHUNK) for c in range(0, T, CHUNK)]
        rounded = [held([P, CHUNK, PACK], BF16, f"rounded{c}") for c in range(len(chunks))]
        last_pair = [held([P, 2, CHUNK], BF16, f"last_pair{c}") for c in range(VECTOR_CHUNKS)]
        out_rows = out_0.rearrange("(p t) c -> p t c", t=PACK)
        for t in range(PACK):
            nc.vector.tensor_copy(planes[t][:].indirect(entries(dst_t, C1, C1)), ys[t][:])
            nc.sync.dma_start(out_rows[:, t, :], planes[t][:])
            for c, cols in enumerate(chunks):
                if t < 2 or c >= VECTOR_CHUNKS:
                    nc.scalar.copy(rounded[c][:, :, t], planes[t][:, cols])
                else:
                    copies[t == PACK - 1](last_pair[c][:, t - 2, :], planes[t][:, cols])
        for c in range(VECTOR_CHUNKS):
            nc.vector.tensor_copy(rounded[c][:, :, 2:PACK], last_pair[c][:].rearrange("p e m -> p m e"))

        out_scales = held([P, T], U8, "out_scales")
        out_words = out_1[0].rearrange("p t d -> p (t d)").bitcast(I32)
        for c, cols in enumerate(chunks):
            codes = held([P, CHUNK], U32, f"out_codes{c}")
            nc.vector.quantize_mx(
                out=codes[:].bitcast(FP8X4),
                scales=out_scales[:, cols],
                in_=rounded[c][:].rearrange("p m t -> p (m t)"),
            )
            nc.sync.dma_start(out_words[:, cols], codes[:].bitcast(I32))
        for q in range(QUADS):
            queue = nc.sync if q % 2 else nc.scalar
            queue.dma_start(out_2[0][4 * q : 4 * q + 4].bitcast(I32), scale_rows(out_scales, q))
